import numpy as np
import ml_dtypes


def mxq(x, axis, fmt="e4m3"):
    dtype, down = {"e4m3": (ml_dtypes.float8_e4m3fn, 7), "e5m2": (ml_dtypes.float8_e5m2, 14)}[fmt]
    v = np.moveaxis(np.asarray(x, np.float32).astype(ml_dtypes.bfloat16).astype(np.float64), axis, -1)
    blocks = v.reshape(v.shape[:-1] + (-1, 32))
    amax = np.abs(blocks).max(-1, keepdims=True)
    byte = np.maximum(np.where(amax > 0, np.frexp(amax)[1] - 1 + 127, 0) - down, 1)
    scale = np.exp2(byte - 127.0)
    codes = (blocks / scale).astype(np.float32).astype(dtype).astype(np.float64)
    return np.moveaxis((codes * scale).reshape(v.shape), -1, axis)


WIDE = False


def mx_kscale(k):
    if not WIDE:
        return np.ones(k)
    levels = np.array([10, -10, 5, -5, 0])
    if k % 512:
        return np.exp2(np.random.permutation(np.resize(levels, k // 32))).repeat(32)
    a = np.empty((k // 512, 16))
    for p in range(k // 512):
        a[p, :8] = np.random.permutation(np.resize(levels, 8))
        for g in range(8):
            far = levels[np.abs(levels - a[p, g]) >= 10]
            a[p, g + 8] = far[np.random.randint(len(far))]
    return np.exp2(a.ravel()).repeat(32)


def f64(x):
    return np.asarray(x).astype(np.float64)


def striped(idx):
    return np.tile(idx.reshape(-1, 16).T, (8, 1)).astype(np.uint16)


def unstriped(offs):
    return offs[:16].T.reshape(-1).astype(np.int64)


def striped8(idx):
    return np.concatenate([x.reshape(-1, 16).T for x in idx]).astype(np.uint16)


def runs(offs, k):
    lists = np.stack([offs[16 * r : 16 * r + 16].T.reshape(-1) for r in range(8)]).astype(np.int64)
    return lists[np.arange(k) % 512 // 64]


def pack_weight(w):
    k, n = w.shape
    w = f64(np.asarray(w, np.float32).astype(ml_dtypes.bfloat16)).reshape(k // 32, 32, n)
    amax = np.abs(w).max(1)
    byte = np.clip(np.where(amax > 0, np.frexp(amax)[1] - 1 + 127 - 7, 1), 1, 254)
    scaled = (w * np.exp2(127.0 - byte)[:, None, :]).reshape(k, n).astype(np.float32)
    words = np.ascontiguousarray(scaled.reshape(k // 512, 128, 4, n).transpose(0, 1, 3, 2)).astype(ml_dtypes.float8_e4m3fn).view(np.uint8)
    return words, np.ascontiguousarray(byte.astype(np.uint8).reshape(k // 512, 16, n))


def unpack_weight(words, scales):
    g, p, n, _ = words.shape
    vals = np.ascontiguousarray(words).view(ml_dtypes.float8_e4m3fn).astype(np.float64) * np.repeat(np.exp2(scales.astype(np.float64) - 127.0), 8, axis=1)[..., None]
    return vals.transpose(0, 1, 3, 2).reshape(g * 512, n)


def sigmoid(v):
    return 1.0 / (1.0 + np.exp(-np.maximum(v, -700.0)))


K, T, S, H, U, C = 512, 2048, 512, 512, 1024, 512


def setup_inputs():
    n = np.random.standard_normal
    s = mx_kscale(K)[:, None]
    packed_xT = pack_weight(n((K, T)) * s)
    return {
        "x_words": packed_xT[0],
        "x_scales": packed_xT[1],
        "w1": (n((K, H)) / np.sqrt(K) / s).astype(np.float32),
        "mem": n((H, U)).astype(np.float32),
        "gs": (np.random.uniform(0.5, 1.5, (K, 1)) / s).astype(np.float32),
        "offs": striped(np.random.permutation(T)[:S]),
        "n1": striped8(np.stack([np.random.permutation(U)[:S] for _ in range(8)])),
        "cand": striped(np.random.permutation(T)[:C]),
        "n2": striped8(np.stack([np.random.permutation(U) for _ in range(8)])),
        "n3": striped8(np.stack([np.random.permutation(U) for _ in range(8)])),
    }


def reference(x_words, x_scales, w1, mem, gs, offs, n1, cand, n2, n3):
    x_cand = unpack_weight(x_words, x_scales)[:, unstriped(cand)]
    old = f64(mem)[np.arange(H)[:, None], runs(n1, H)]
    xq = unpack_weight(x_words, x_scales)[:, unstriped(offs)]
    y = mxq(f64(w1), 0, "e4m3").T @ xq
    nw = old + sigmoid(y) * (y - old)
    pg = f64(mem).copy()
    pg[np.arange(H)[:, None], runs(n1, H)] = nw
    z = f64(gs) * pg
    s = 0.0625 * ((x_cand.T @ mxq(z, 0, "e4m3")))
    return (s[np.arange(C)[:, None], runs(n2, C)]) / (np.abs(s) + np.abs(s[np.arange(C)[:, None], runs(n3, C)]) + 0.5)

@@ -1,0 +1,257 @@
+from contextlib import ExitStack
+
+import concourse.mybir as mybir
+
+K, T, S, H, U, C = 512, 2048, 512, 512, 1024, 512
+FLOPS = 2 * K * H * S + 2 * K * C * U
+
+F32 = mybir.dt.float32
+BF16 = mybir.dt.bfloat16
+I32 = mybir.dt.int32
+U32 = mybir.dt.uint32
+U16 = mybir.dt.uint16
+U8 = mybir.dt.uint8
+FP8X4 = mybir.dt.float8_e4m3fn_x4
+ACT = mybir.ActivationFunctionType
+ALU = mybir.AluOpType
+
+P = 128
+PACK = 4
+BANK = 512
+HALVES = U // BANK
+LANES = 16
+
+
+def tile_picked_candpagetnorm2_none_p_kernel(
+    tc, x_words, x_scales, w1, mem, gs, offs, n1, cand, n2, n3, out
+):
+    nc = tc.nc
+    with ExitStack() as ctx:
+        keep = ctx.enter_context(tc.tile_pool(name="keep", bufs=1))
+        ring = ctx.enter_context(tc.tile_pool(name="ring", bufs=2))
+        psum = ctx.enter_context(tc.psum_pool(name="psum", bufs=1))
+
+        def bank(b):
+            return psum.tile([P, BANK], F32, name="bank%d" % b, tag="bank%d" % b)
+
+        def half(h):
+            return slice(h * BANK, (h + 1) * BANK)
+
+        offs_t = keep.tile([P, S // LANES], U16, name="offs_t")
+        n1_t = keep.tile([P, S // LANES], U16, name="n1_t")
+        cand_t = keep.tile([P, C // LANES], U16, name="cand_t")
+        n2_t = keep.tile([P, U // LANES], U16, name="n2_t")
+        n3_t = keep.tile([P, U // LANES], U16, name="n3_t")
+        xw = keep.tile([P, T], U32, name="xw", align_bytes=64)
+        xs = keep.tile([P, T], U8, name="xs", align_bytes=64)
+        w_raw = [keep.tile([P, PACK, H // 2], F32, name="w_raw%d" % h) for h in range(2)]
+        page = [keep.tile([P, U], F32, name="page%d" % t) for t in range(PACK)]
+        gain = keep.tile([P, PACK], F32, name="gain")
+        one = keep.tile([P, 1], F32, name="one")
+        warm = keep.tile([P, 1], F32, name="warm")
+        order = (2, 0, 1, 3)
+
+        nc.vector.memset(xs[:].bitcast(I32), 0)
+        nc.gpsimd.memset(one[:], 1.0)
+
+        nc.sync.dma_start(xw[:].bitcast(I32), x_words[0].rearrange("p n t -> p (n t)").bitcast(I32))
+        nc.sync.dma_start(offs_t[:], offs)
+        for q in range(4):
+            nc.scalar.dma_start(
+                xs[32 * q : 32 * q + 4, :].bitcast(I32), x_scales[0, 4 * q : 4 * q + 4, :].bitcast(I32)
+            )
+        nc.scalar.activation(warm[:], one[:], ACT.Silu)
+        w_rows = w1.rearrange("(p j) c -> p j c", j=PACK)
+        for h in range(2):
+            nc.sync.dma_start(w_raw[h][:], w_rows[:, :, h * (H // 2) : (h + 1) * (H // 2)])
+        nc.sync.dma_start(cand_t[:], cand)
+        mem_rows = mem.rearrange("(p t) w -> t p w", t=PACK)
+        nc.sync.dma_start(n1_t[:], n1)
+        for t in order:
+            nc.sync.dma_start(page[t][:], mem_rows[t])
+        nc.sync.dma_start(gain[:], gs.rearrange("(p t) o -> p (t o)", t=PACK))
+        nc.sync.dma_start(n3_t[:], n3)
+        nc.sync.dma_start(n2_t[:], n2)
+
+        xq_w = keep.tile([P, S], U32, name="xq_w", align_bytes=64)
+        xq_s = keep.tile([P, S], U8, name="xq_s", align_bytes=64)
+        cand_raw = keep.tile([P, C], U8, name="cand_raw", align_bytes=64)
+        cand_s = keep.tile([P, C], U8, name="cand_s", align_bytes=64)
+        nc.vector.tensor_copy(xq_w[:], xw[:].indirect(offs_t[:]))
+        nc.vector.tensor_copy(xq_s[:], xs[:].indirect(offs_t[:]))
+        nc.vector.tensor_copy(cand_raw[:], xs[:].indirect(cand_t[:]))
+
+        w_bf = keep.tile([P, PACK, P, PACK], BF16, name="w_bf", tag="w_then_cand", align_bytes=64)
+
+        def weave(copy, h, lo, hi):
+            copy(
+                w_bf[:, :, h * (P // 2) + lo : h * (P // 2) + hi, :].rearrange("p t m j -> p m j t"),
+                w_raw[h][:, :, lo * PACK : hi * PACK].rearrange("p j (m t) -> p m j t", t=PACK),
+            )
+
+        weave(nc.scalar.copy, 0, 0, P // 2)
+        weave(nc.scalar.copy, 1, 0, P // 2)
+        w_codes = keep.tile([P, H], U32, name="w_codes", align_bytes=64)
+        w_scales = keep.tile([P, H], U8, name="w_scales", align_bytes=64)
+        for lo, hi in ((2, 3), (0, 2), (3, 4)):
+            nc.vector.quantize_mx(
+                out=w_codes[:, lo * P : hi * P].bitcast(FP8X4),
+                scales=w_scales[:, lo * P : hi * P],
+                in_=w_bf[:, lo:hi].rearrange("p t m j -> p (t m j)"),
+            )
+
+        th, fresh, hold = {}, {}, {}
+
+        def holding(t):
+            hold[t] = keep.tile([P, S], F32, name="hold")
+            nc.scalar.activation(hold[t][:], th[t][:], ACT.Copy, scale=0.5, bias=0.5)
+
+        for t in order:
+            y = bank(t)
+            cols = slice(t * P, (t + 1) * P)
+            nc.tensor.matmul_mx(
+                out=y[:],
+                lhsT=w_codes[:, cols].bitcast(FP8X4),
+                lhsT_scale=w_scales[:, cols],
+                rhs=xq_w[:].bitcast(FP8X4),
+                rhs_scale=xq_s[:],
+                start=True,
+                stop=True,
+            )
+            th[t] = keep.tile([P, S], F32, name="th%d" % t)
+            fresh[t] = keep.tile([P, S], F32, name="fresh%d" % t)
+            nc.scalar.activation(th[t][:], y[:], ACT.Tanh, scale=-0.5)
+            if t == order[1]:
+                holding(t)
+            nc.scalar.activation(fresh[t][:], y[:], ACT.Silu)
+
+        z_bf = [keep.tile([P, BANK, PACK], BF16, name="z_bf%d" % h, align_bytes=64) for h in range(HALVES)]
+        z_codes, z_scales = [], []
+        for i, t in enumerate(order):
+            kept = ring.tile([P, S], F32, name="kept")
+            if i == 0:
+                half_old = keep.tile([P, S], F32, name="half_old")
+                nc.vector.tensor_scalar(half_old[:], page[t][:].indirect(n1_t[:]), 0.5, 0.0, ALU.mult, ALU.add)
+                nc.vector.scalar_tensor_tensor(kept[:], th[t][:], 1.0, half_old[:], ALU.add, ALU.mult)
+            else:
+                nc.vector.tensor_tensor(kept[:], page[t][:].indirect(n1_t[:]), hold[t][:], ALU.mult)
+                if i + 1 < PACK:
+                    holding(order[i + 1])
+            nc.vector.tensor_tensor(page[t][:].indirect(n1_t[:]), kept[:], fresh[t][:], ALU.add)
+            last = i == PACK - 1
+            if i == 0:
+                cand_w = keep.tile([P, C], U32, name="cand_w", tag="w_then_cand", align_bytes=64)
+                nc.vector.tensor_copy(
+                    cand_w[:].rearrange("p (t b e) -> p b t e", t=PACK, e=PACK), xw[:].indirect(cand_t[:])
+                )
+                nc.vector.tensor_copy(
+                    cand_s[:].bitcast(I32).rearrange("p (t b) -> p b t", t=PACK),
+                    cand_raw[:].bitcast(I32).rearrange("p (b t) -> p b t", t=PACK),
+                )
+            if i == 2:
+                warm2 = keep.tile([P, 1], F32, name="warm2")
+                nc.scalar.activation(warm2[:], hold[order[3]][:, 0:1], ACT.Abs_reciprocal_sqrt, bias=1.0)
+            for h in range(HALVES):
+                if last and h == 0:
+                    nc.vector.tensor_scalar(z_bf[h][:, :, t], page[t][:, half(h)], gain[:, t : t + 1], None, ALU.mult)
+                else:
+                    nc.scalar.activation(z_bf[h][:, :, t], page[t][:, half(h)], ACT.Copy, scale=gain[:, t : t + 1])
+                if last:
+                    zc = keep.tile([P, BANK], U32, name="z_codes%d" % h, align_bytes=64)
+                    zs = keep.tile([P, BANK], U8, name="z_scales%d" % h, align_bytes=64)
+                    nc.vector.quantize_mx(
+                        out=zc[:].bitcast(FP8X4), scales=zs[:], in_=z_bf[h][:].rearrange("p w t -> p (w t)")
+                    )
+                    z_codes.append(zc)
+                    z_scales.append(zs)
+
+        out_rows = out.rearrange("(b t e) w -> t b e w", t=PACK, e=PACK)
+        size = [keep.tile([P, U], F32, name="size%d" % t) for t in range(PACK)]
+        signed = [keep.tile([P, U], F32, name="signed%d" % t) for t in range(PACK)]
+        acc, twin, total, recip = {}, {}, {}, {}
+        for t in range(PACK):
+            cols = slice(t * P, (t + 1) * P)
+            for h in range(HALVES):
+                acc[t, h] = bank(2 * t + h)
+                nc.tensor.matmul_mx(
+                    out=acc[t, h][:],
+                    lhsT=cand_w[:, cols].bitcast(FP8X4),
+                    lhsT_scale=cand_s[:, cols],
+                    rhs=z_codes[h][:].bitcast(FP8X4),
+                    rhs_scale=z_scales[h][:],
+                    start=True,
+                    stop=True,
+                )
+                twin[t, h] = keep.tile([P, BANK], F32, name="twin%d%d" % (t, h))
+
+        def entries(h):
+            return slice(h * BANK // LANES, (h + 1) * BANK // LANES)
+
+        def sizes(t, h):
+            nc.scalar.activation(size[t][:, half(h)], acc[t, h][:], ACT.Abs, scale=0.0625)
+
+        def signs(t, h):
+            nc.scalar.activation(signed[t][:, half(h)], acc[t, h][:], ACT.Copy, scale=0.0625)
+
+        def gather_total(t, h):
+            total[t, h] = keep.tile([P, BANK], F32, name="total%d%d" % (t, h))
+            nc.vector.tensor_tensor(total[t, h][:], size[t][:].indirect(n3_t[:, entries(h)]), twin[t, h][:], ALU.add)
+
+        def invert(t, h):
+            root = ring.tile([P, BANK], F32, name="root")
+            nc.scalar.activation(root[:], total[t, h][:], ACT.Abs_reciprocal_sqrt, bias=0.5)
+            recip[t, h] = keep.tile([P, BANK], F32, name="recip%d%d" % (t, h))
+            nc.scalar.activation(recip[t, h][:], root[:], ACT.Square)
+
+        def finish(t, h):
+            res = ring.tile([P, BANK], F32, name="res", bufs=4)
+            pieces = 2 if (t, h) == (PACK - 1, HALVES - 1) else 1
+            width = BANK // pieces
+            for c in range(pieces):
+                lo = h * BANK + c * width
+                part = slice(c * width, (c + 1) * width)
+                nc.vector.tensor_tensor(
+                    res[:, part],
+                    signed[t][:].indirect(n2_t[:, lo // LANES : (lo + width) // LANES]),
+                    recip[t, h][:, part],
+                    ALU.mult,
+                )
+                nc.sync.dma_start(out_rows[t][:, :, lo : lo + width], res[:, part])
+
+        def twin_by_dma(t, h):
+            nc.sync.dma_start(twin[t, h][:], size[t][:, half(h)])
+
+        sizes(0, 0)
+        nc.vector.tensor_scalar(signed[0][:, half(0)], acc[0, 0][:], 0.0625, None, ALU.mult)
+        nc.vector.tensor_copy(twin[0, 0][:], size[0][:, half(0)])
+        sizes(0, 1)
+        gather_total(0, 0)
+        nc.vector.tensor_copy(twin[0, 1][:], size[0][:, half(1)])
+        gather_total(0, 1)
+        sizes(1, 0)
+        sizes(1, 1)
+        twin_by_dma(1, 1)
+        nc.scalar.activation(twin[1, 0][:], acc[1, 0][:], ACT.Abs, scale=0.0625)
+        gather_total(1, 0)
+        gather_total(1, 1)
+        for h in range(HALVES):
+            sizes(2, h)
+            twin_by_dma(2, h)
+        signs(0, 1)
+        invert(0, 0)
+        finish(0, 0)
+        for h in range(HALVES):
+            gather_total(2, h)
+        for h in range(HALVES):
+            sizes(3, h)
+            twin_by_dma(3, h)
+        invert(0, 1)
+        finish(0, 1)
+        for h in range(HALVES):
+            gather_total(3, h)
+        for t in range(1, PACK):
+            for h in range(HALVES):
+                signs(t, h)
+            for h in range(HALVES):
+                invert(t, h)
+                finish(t, h)

@@ -54,19 +54,19 @@ def tile_picked_candpagetnorm2_none_p_kernel(
         nc.vector.memset(xs[:].bitcast(I32), 0)
         nc.gpsimd.memset(one[:], 1.0)
 
-        nc.sync.dma_start(xw[:].bitcast(I32), x_words[0].rearrange("p n t -> p (n t)").bitcast(I32))
         nc.sync.dma_start(offs_t[:], offs)
+        nc.sync.dma_start(cand_t[:], cand)
+        nc.sync.dma_start(n1_t[:], n1)
         for q in range(4):
-            nc.scalar.dma_start(
+            nc.sync.dma_start(
                 xs[32 * q : 32 * q + 4, :].bitcast(I32), x_scales[0, 4 * q : 4 * q + 4, :].bitcast(I32)
             )
+        nc.sync.dma_start(xw[:].bitcast(I32), x_words[0].rearrange("p n t -> p (n t)").bitcast(I32))
         nc.scalar.activation(warm[:], one[:], ACT.Silu)
         w_rows = w1.rearrange("(p j) c -> p j c", j=PACK)
         for h in range(2):
             nc.sync.dma_start(w_raw[h][:], w_rows[:, :, h * (H // 2) : (h + 1) * (H // 2)])
-        nc.sync.dma_start(cand_t[:], cand)
         mem_rows = mem.rearrange("(p t) w -> t p w", t=PACK)
-        nc.sync.dma_start(n1_t[:], n1)
         for t in order:
             nc.sync.dma_start(page[t][:], mem_rows[t])
         nc.sync.dma_start(gain[:], gs.rearrange("(p t) o -> p (t o)", t=PACK))
@@ -77,11 +77,19 @@ def tile_picked_candpagetnorm2_none_p_kernel(
         xq_s = keep.tile([P, S], U8, name="xq_s", align_bytes=64)
         cand_raw = keep.tile([P, C], U8, name="cand_raw", align_bytes=64)
         cand_s = keep.tile([P, C], U8, name="cand_s", align_bytes=64)
-        nc.vector.tensor_copy(xq_w[:], xw[:].indirect(offs_t[:]))
+        cand_w = keep.tile([P, C], U32, name="cand_w", align_bytes=64)
         nc.vector.tensor_copy(xq_s[:], xs[:].indirect(offs_t[:]))
         nc.vector.tensor_copy(cand_raw[:], xs[:].indirect(cand_t[:]))
+        nc.vector.tensor_copy(xq_w[:], xw[:].indirect(offs_t[:]))
+        nc.vector.tensor_copy(
+            cand_w[:].rearrange("p (t b e) -> p b t e", t=PACK, e=PACK), xw[:].indirect(cand_t[:])
+        )
+        nc.vector.tensor_copy(
+            cand_s[:].bitcast(I32).rearrange("p (t b) -> p b t", t=PACK),
+            cand_raw[:].bitcast(I32).rearrange("p (b t) -> p b t", t=PACK),
+        )
 
-        w_bf = keep.tile([P, PACK, P, PACK], BF16, name="w_bf", tag="w_then_cand", align_bytes=64)
+        w_bf = keep.tile([P, PACK, P, PACK], BF16, name="w_bf", align_bytes=64)
 
         def weave(copy, h, lo, hi):
             copy(
@@ -90,7 +98,8 @@ def tile_picked_candpagetnorm2_none_p_kernel(
             )
 
         weave(nc.scalar.copy, 0, 0, P // 2)
-        weave(nc.scalar.copy, 1, 0, P // 2)
+        weave(nc.scalar.copy, 1, 0, P // 4)
+        weave(nc.vector.tensor_copy, 1, P // 4, P // 2)
         w_codes = keep.tile([P, H], U32, name="w_codes", align_bytes=64)
         w_scales = keep.tile([P, H], U8, name="w_scales", align_bytes=64)
         for lo, hi in ((2, 3), (0, 2), (3, 4)):
@@ -100,17 +109,12 @@ def tile_picked_candpagetnorm2_none_p_kernel(
                 in_=w_bf[:, lo:hi].rearrange("p t m j -> p (t m j)"),
             )
 
-        th, fresh, hold = {}, {}, {}
-
-        def holding(t):
-            hold[t] = keep.tile([P, S], F32, name="hold")
-            nc.scalar.activation(hold[t][:], th[t][:], ACT.Copy, scale=0.5, bias=0.5)
-
+        y, th, fresh, kept = {}, {}, {}, {}
         for t in order:
-            y = bank(t)
+            y[t] = bank(t)
             cols = slice(t * P, (t + 1) * P)
             nc.tensor.matmul_mx(
-                out=y[:],
+                out=y[t][:],
                 lhsT=w_codes[:, cols].bitcast(FP8X4),
                 lhsT_scale=w_scales[:, cols],
                 rhs=xq_w[:].bitcast(FP8X4),
@@ -118,71 +122,100 @@ def tile_picked_candpagetnorm2_none_p_kernel(
                 start=True,
                 stop=True,
             )
-            th[t] = keep.tile([P, S], F32, name="th%d" % t)
-            fresh[t] = keep.tile([P, S], F32, name="fresh%d" % t)
-            nc.scalar.activation(th[t][:], y[:], ACT.Tanh, scale=-0.5)
-            if t == order[1]:
-                holding(t)
-            nc.scalar.activation(fresh[t][:], y[:], ACT.Silu)
-
         z_bf = [keep.tile([P, BANK, PACK], BF16, name="z_bf%d" % h, align_bytes=64) for h in range(HALVES)]
-        z_codes, z_scales = [], []
-        for i, t in enumerate(order):
-            kept = ring.tile([P, S], F32, name="kept")
-            if i == 0:
-                half_old = keep.tile([P, S], F32, name="half_old")
-                nc.vector.tensor_scalar(half_old[:], page[t][:].indirect(n1_t[:]), 0.5, 0.0, ALU.mult, ALU.add)
-                nc.vector.scalar_tensor_tensor(kept[:], th[t][:], 1.0, half_old[:], ALU.add, ALU.mult)
-            else:
-                nc.vector.tensor_tensor(kept[:], page[t][:].indirect(n1_t[:]), hold[t][:], ALU.mult)
-                if i + 1 < PACK:
-                    holding(order[i + 1])
-            nc.vector.tensor_tensor(page[t][:].indirect(n1_t[:]), kept[:], fresh[t][:], ALU.add)
-            last = i == PACK - 1
-            if i == 0:
-                cand_w = keep.tile([P, C], U32, name="cand_w", tag="w_then_cand", align_bytes=64)
-                nc.vector.tensor_copy(
-                    cand_w[:].rearrange("p (t b e) -> p b t e", t=PACK, e=PACK), xw[:].indirect(cand_t[:])
-                )
-                nc.vector.tensor_copy(
-                    cand_s[:].bitcast(I32).rearrange("p (t b) -> p b t", t=PACK),
-                    cand_raw[:].bitcast(I32).rearrange("p (b t) -> p b t", t=PACK),
-                )
-            if i == 2:
-                warm2 = keep.tile([P, 1], F32, name="warm2")
-                nc.scalar.activation(warm2[:], hold[order[3]][:, 0:1], ACT.Abs_reciprocal_sqrt, bias=1.0)
+
+        def gate(t):
+            th[t] = keep.tile([P, S], F32, name="th%d" % t)
+            nc.scalar.activation(th[t][:], y[t][:], ACT.Tanh, scale=-0.5)
+
+        def new_part(t):
+            fresh[t] = keep.tile([P, S], F32, name="fresh%d" % t)
+            nc.scalar.activation(fresh[t][:], y[t][:], ACT.Silu)
+
+        def old_part(t):
+            gate(t)
+            hold = keep.tile([P, S], F32, name="hold%d" % t)
+            nc.scalar.activation(hold[:], th[t][:], ACT.Copy, scale=0.5, bias=0.5)
+            kept[t] = keep.tile([P, S], F32, name="kept%d" % t)
+            nc.vector.tensor_tensor(kept[t][:], page[t][:].indirect(n1_t[:]), hold[:], ALU.mult)
+
+        def put(t):
+            nc.vector.tensor_tensor(page[t][:].indirect(n1_t[:]), kept[t][:], fresh[t][:], ALU.add)
+
+        def plane(t):
             for h in range(HALVES):
-                if last and h == 0:
-                    nc.vector.tensor_scalar(z_bf[h][:, :, t], page[t][:, half(h)], gain[:, t : t + 1], None, ALU.mult)
-                else:
-                    nc.scalar.activation(z_bf[h][:, :, t], page[t][:, half(h)], ACT.Copy, scale=gain[:, t : t + 1])
-                if last:
-                    zc = keep.tile([P, BANK], U32, name="z_codes%d" % h, align_bytes=64)
-                    zs = keep.tile([P, BANK], U8, name="z_scales%d" % h, align_bytes=64)
-                    nc.vector.quantize_mx(
-                        out=zc[:].bitcast(FP8X4), scales=zs[:], in_=z_bf[h][:].rearrange("p w t -> p (w t)")
-                    )
-                    z_codes.append(zc)
-                    z_scales.append(zs)
+                nc.scalar.activation(z_bf[h][:, :, t], page[t][:, half(h)], ACT.Copy, scale=gain[:, t : t + 1])
+
+        a, b, c, d = order
+        gate(a)
+        new_part(a)
+        half_old = keep.tile([P, S], F32, name="half_old")
+        kept[a] = keep.tile([P, S], F32, name="kept_first")
+        nc.vector.tensor_scalar(half_old[:], page[a][:].indirect(n1_t[:]), 0.5, 0.0, ALU.mult, ALU.add)
+        nc.vector.scalar_tensor_tensor(kept[a][:], th[a][:], 1.0, half_old[:], ALU.add, ALU.mult)
+        put(a)
+        old_part(b)
+        old_part(c)
+        new_part(b)
+        put(b)
+        old_part(d)
+        plane(a)
+        new_part(c)
+        put(c)
+        new_part(d)
+        put(d)
+        plane(b)
+        plane(c)
+        t = order[-1]
+        QUARTER = BANK // 2
+        for c in range(2):
+            part = slice(c * QUARTER, (c + 1) * QUARTER)
+            nc.vector.tensor_scalar(z_bf[0][:, part, t], page[t][:, half(0)][:, part], gain[:, t : t + 1], None, ALU.mult)
+            nc.scalar.activation(z_bf[1][:, part, t], page[t][:, half(1)][:, part], ACT.Copy, scale=gain[:, t : t + 1])
+        z_codes = [keep.tile([P, BANK], U32, name="z_codes%d" % h, align_bytes=64) for h in range(HALVES)]
+        z_scales = [keep.tile([P, BANK], U8, name="z_scales%d" % h, align_bytes=64) for h in range(HALVES)]
+        for c in range(2):
+            part = slice(c * QUARTER, (c + 1) * QUARTER)
+            for h in range(HALVES):
+                nc.vector.quantize_mx(
+                    out=z_codes[h][:, part].bitcast(FP8X4),
+                    scales=z_scales[h][:, part],
+                    in_=z_bf[h][:, part, :].rearrange("p w t -> p (w t)"),
+                )
 
         out_rows = out.rearrange("(b t e) w -> t b e w", t=PACK, e=PACK)
         size = [keep.tile([P, U], F32, name="size%d" % t) for t in range(PACK)]
         signed = [keep.tile([P, U], F32, name="signed%d" % t) for t in range(PACK)]
         acc, twin, total, recip = {}, {}, {}, {}
         for t in range(PACK):
-            cols = slice(t * P, (t + 1) * P)
             for h in range(HALVES):
-                acc[t, h] = bank(2 * t + h)
-                nc.tensor.matmul_mx(
-                    out=acc[t, h][:],
-                    lhsT=cand_w[:, cols].bitcast(FP8X4),
-                    lhsT_scale=cand_s[:, cols],
-                    rhs=z_codes[h][:].bitcast(FP8X4),
-                    rhs_scale=z_scales[h][:],
-                    start=True,
-                    stop=True,
-                )
                 twin[t, h] = keep.tile([P, BANK], F32, name="twin%d%d" % (t, h))
+
+        def score(result, t, h, part):
+            cols = slice(t * P, (t + 1) * P)
+            nc.tensor.matmul_mx(
+                out=result,
+                lhsT=cand_w[:, cols].bitcast(FP8X4),
+                lhsT_scale=cand_s[:, cols],
+                rhs=z_codes[h][:, part].bitcast(FP8X4),
+                rhs_scale=z_scales[h][:, part],
+                start=True,
+                stop=True,
+            )
+
+        first = {}
+        for c in range(2):
+            part = slice(c * QUARTER, (c + 1) * QUARTER)
+            for h in range(HALVES):
+                first[c, h] = bank(2 * c + h)
+                score(first[c, h][:, :QUARTER], 0, h, part)
+                nc.scalar.activation(size[0][:, half(h)][:, part], first[c, h][:, :QUARTER], ACT.Abs, scale=0.0625)
+        for h in range(HALVES):
+            nc.vector.tensor_scalar(signed[0][:, half(h)][:, :QUARTER], first[0, h][:, :QUARTER], 0.0625, None, ALU.mult)
+        for t in range(1, PACK):
+            for h in range(HALVES):
+                acc[t, h] = bank((2 * t + 2 + h) % 8)
+                score(acc[t, h][:], t, h, slice(0, BANK))
 
         def entries(h):
             return slice(h * BANK // LANES, (h + 1) * BANK // LANES)
@@ -205,11 +238,10 @@ def tile_picked_candpagetnorm2_none_p_kernel(
 
         def finish(t, h):
             res = ring.tile([P, BANK], F32, name="res", bufs=4)
-            pieces = 2 if (t, h) == (PACK - 1, HALVES - 1) else 1
-            width = BANK // pieces
-            for c in range(pieces):
-                lo = h * BANK + c * width
-                part = slice(c * width, (c + 1) * width)
+            cuts = (0, 384, BANK) if (t, h) == (PACK - 1, HALVES - 1) else (0, BANK)
+            for first, end in zip(cuts, cuts[1:]):
+                lo, width = h * BANK + first, end - first
+                part = slice(first, end)
                 nc.vector.tensor_tensor(
                     res[:, part],
                     signed[t][:].indirect(n2_t[:, lo // LANES : (lo + width) // LANES]),
@@ -221,37 +253,27 @@ def tile_picked_candpagetnorm2_none_p_kernel(
         def twin_by_dma(t, h):
             nc.sync.dma_start(twin[t, h][:], size[t][:, half(h)])
 
-        sizes(0, 0)
-        nc.vector.tensor_scalar(signed[0][:, half(0)], acc[0, 0][:], 0.0625, None, ALU.mult)
-        nc.vector.tensor_copy(twin[0, 0][:], size[0][:, half(0)])
-        sizes(0, 1)
-        gather_total(0, 0)
-        nc.vector.tensor_copy(twin[0, 1][:], size[0][:, half(1)])
-        gather_total(0, 1)
-        sizes(1, 0)
-        sizes(1, 1)
-        twin_by_dma(1, 1)
-        nc.scalar.activation(twin[1, 0][:], acc[1, 0][:], ACT.Abs, scale=0.0625)
-        gather_total(1, 0)
-        gather_total(1, 1)
         for h in range(HALVES):
-            sizes(2, h)
-            twin_by_dma(2, h)
-        signs(0, 1)
-        invert(0, 0)
-        finish(0, 0)
+            nc.vector.tensor_copy(twin[0, h][:], size[0][:, half(h)])
         for h in range(HALVES):
-            gather_total(2, h)
-        for h in range(HALVES):
-            sizes(3, h)
-            twin_by_dma(3, h)
-        invert(0, 1)
-        finish(0, 1)
-        for h in range(HALVES):
-            gather_total(3, h)
+            gather_total(0, h)
         for t in range(1, PACK):
             for h in range(HALVES):
-                signs(t, h)
+                sizes(t, h)
+                if (t, h) != (1, 0):
+                    twin_by_dma(t, h)
+        nc.vector.tensor_copy(twin[1, 0][:], size[1][:, half(0)])
+        for t in range(1, PACK):
+            for h in range(HALVES):
+                gather_total(t, h)
+        for h in range(HALVES):
+            nc.scalar.activation(
+                signed[0][:, half(h)][:, QUARTER:], first[1, h][:, :QUARTER], ACT.Copy, scale=0.0625
+            )
+        for t in range(PACK):
+            for h in range(HALVES):
+                if t > 0:
+                    signs(t, h)
             for h in range(HALVES):
                 invert(t, h)
                 finish(t, h)

@@ -56,16 +56,16 @@ def tile_picked_candpagetnorm2_none_p_kernel(
 
         nc.sync.dma_start(offs_t[:], offs)
         nc.sync.dma_start(cand_t[:], cand)
-        nc.sync.dma_start(n1_t[:], n1)
+        w_rows = w1.rearrange("(p j) c -> p j c", j=PACK)
+        nc.sync.dma_start(w_raw[0][:], w_rows[:, :, : H // 2])
         for q in range(4):
             nc.sync.dma_start(
                 xs[32 * q : 32 * q + 4, :].bitcast(I32), x_scales[0, 4 * q : 4 * q + 4, :].bitcast(I32)
             )
         nc.sync.dma_start(xw[:].bitcast(I32), x_words[0].rearrange("p n t -> p (n t)").bitcast(I32))
         nc.scalar.activation(warm[:], one[:], ACT.Silu)
-        w_rows = w1.rearrange("(p j) c -> p j c", j=PACK)
-        for h in range(2):
-            nc.sync.dma_start(w_raw[h][:], w_rows[:, :, h * (H // 2) : (h + 1) * (H // 2)])
+        nc.sync.dma_start(w_raw[1][:], w_rows[:, :, H // 2 :])
+        nc.sync.dma_start(n1_t[:], n1)
         mem_rows = mem.rearrange("(p t) w -> t p w", t=PACK)
         for t in order:
             nc.sync.dma_start(page[t][:], mem_rows[t])
@@ -98,8 +98,7 @@ def tile_picked_candpagetnorm2_none_p_kernel(
             )
 
         weave(nc.scalar.copy, 0, 0, P // 2)
-        weave(nc.scalar.copy, 1, 0, P // 4)
-        weave(nc.vector.tensor_copy, 1, P // 4, P // 2)
+        weave(nc.scalar.copy, 1, 0, P // 2)
         w_codes = keep.tile([P, H], U32, name="w_codes", align_bytes=64)
         w_scales = keep.tile([P, H], U8, name="w_scales", align_bytes=64)
         for lo, hi in ((2, 3), (0, 2), (3, 4)):
@@ -253,16 +252,17 @@ def tile_picked_candpagetnorm2_none_p_kernel(
         def twin_by_dma(t, h):
             nc.sync.dma_start(twin[t, h][:], size[t][:, half(h)])
 
-        for h in range(HALVES):
-            nc.vector.tensor_copy(twin[0, h][:], size[0][:, half(h)])
-        for h in range(HALVES):
-            gather_total(0, h)
+        nc.vector.tensor_copy(twin[0, 0][:], size[0][:, half(0)])
+        gather_total(0, 0)
+        sizes(1, 0)
+        nc.vector.tensor_copy(twin[1, 0][:], size[1][:, half(0)])
+        nc.scalar.copy(twin[0, 1][:], size[0][:, half(1)])
+        gather_total(0, 1)
         for t in range(1, PACK):
             for h in range(HALVES):
-                sizes(t, h)
                 if (t, h) != (1, 0):
+                    sizes(t, h)
                     twin_by_dma(t, h)
-        nc.vector.tensor_copy(twin[1, 0][:], size[1][:, half(0)])
         for t in range(1, PACK):
             for h in range(HALVES):
                 gather_total(t, h)

@@ -56,16 +56,16 @@ def tile_picked_candpagetnorm2_none_p_kernel(
 
         nc.sync.dma_start(offs_t[:], offs)
         nc.sync.dma_start(cand_t[:], cand)
-        w_rows = w1.rearrange("(p j) c -> p j c", j=PACK)
-        nc.sync.dma_start(w_raw[0][:], w_rows[:, :, : H // 2])
+        nc.sync.dma_start(n1_t[:], n1)
         for q in range(4):
             nc.sync.dma_start(
                 xs[32 * q : 32 * q + 4, :].bitcast(I32), x_scales[0, 4 * q : 4 * q + 4, :].bitcast(I32)
             )
         nc.sync.dma_start(xw[:].bitcast(I32), x_words[0].rearrange("p n t -> p (n t)").bitcast(I32))
         nc.scalar.activation(warm[:], one[:], ACT.Silu)
-        nc.sync.dma_start(w_raw[1][:], w_rows[:, :, H // 2 :])
-        nc.sync.dma_start(n1_t[:], n1)
+        w_rows = w1.rearrange("(p j) c -> p j c", j=PACK)
+        for h in range(2):
+            nc.sync.dma_start(w_raw[h][:], w_rows[:, :, h * (H // 2) : (h + 1) * (H // 2)])
         mem_rows = mem.rearrange("(p t) w -> t p w", t=PACK)
         for t in order:
             nc.sync.dma_start(page[t][:], mem_rows[t])
@@ -98,7 +98,8 @@ def tile_picked_candpagetnorm2_none_p_kernel(
             )
 
         weave(nc.scalar.copy, 0, 0, P // 2)
-        weave(nc.scalar.copy, 1, 0, P // 2)
+        weave(nc.scalar.copy, 1, 0, P // 4)
+        weave(nc.vector.tensor_copy, 1, P // 4, P // 2)
         w_codes = keep.tile([P, H], U32, name="w_codes", align_bytes=64)
         w_scales = keep.tile([P, H], U8, name="w_scales", align_bytes=64)
         for lo, hi in ((2, 3), (0, 2), (3, 4)):
@@ -132,7 +133,6 @@ def tile_picked_candpagetnorm2_none_p_kernel(
             nc.scalar.activation(fresh[t][:], y[t][:], ACT.Silu)
 
         def old_part(t):
-            gate(t)
             hold = keep.tile([P, S], F32, name="hold%d" % t)
             nc.scalar.activation(hold[:], th[t][:], ACT.Copy, scale=0.5, bias=0.5)
             kept[t] = keep.tile([P, S], F32, name="kept%d" % t)
@@ -141,9 +141,8 @@ def tile_picked_candpagetnorm2_none_p_kernel(
         def put(t):
             nc.vector.tensor_tensor(page[t][:].indirect(n1_t[:]), kept[t][:], fresh[t][:], ALU.add)
 
-        def plane(t):
-            for h in range(HALVES):
-                nc.scalar.activation(z_bf[h][:, :, t], page[t][:, half(h)], ACT.Copy, scale=gain[:, t : t + 1])
+        def plane(t, h):
+            nc.scalar.activation(z_bf[h][:, :, t], page[t][:, half(h)], ACT.Copy, scale=gain[:, t : t + 1])
 
         a, b, c, d = order
         gate(a)
@@ -153,18 +152,23 @@ def tile_picked_candpagetnorm2_none_p_kernel(
         nc.vector.tensor_scalar(half_old[:], page[a][:].indirect(n1_t[:]), 0.5, 0.0, ALU.mult, ALU.add)
         nc.vector.scalar_tensor_tensor(kept[a][:], th[a][:], 1.0, half_old[:], ALU.add, ALU.mult)
         put(a)
+        gate(b)
+        gate(c)
         old_part(b)
         old_part(c)
+        gate(d)
         new_part(b)
         put(b)
         old_part(d)
-        plane(a)
+        plane(a, 0)
+        plane(a, 1)
         new_part(c)
         put(c)
         new_part(d)
         put(d)
-        plane(b)
-        plane(c)
+        for t in (b, c):
+            for h in range(HALVES):
+                plane(t, h)
         t = order[-1]
         QUARTER = BANK // 2
         for c in range(2):
@@ -185,7 +189,7 @@ def tile_picked_candpagetnorm2_none_p_kernel(
         out_rows = out.rearrange("(b t e) w -> t b e w", t=PACK, e=PACK)
         size = [keep.tile([P, U], F32, name="size%d" % t) for t in range(PACK)]
         signed = [keep.tile([P, U], F32, name="signed%d" % t) for t in range(PACK)]
-        acc, twin, total, recip = {}, {}, {}, {}
+        acc, twin, total, root = {}, {}, {}, {}
         for t in range(PACK):
             for h in range(HALVES):
                 twin[t, h] = keep.tile([P, BANK], F32, name="twin%d%d" % (t, h))
@@ -229,34 +233,31 @@ def tile_picked_candpagetnorm2_none_p_kernel(
             total[t, h] = keep.tile([P, BANK], F32, name="total%d%d" % (t, h))
             nc.vector.tensor_tensor(total[t, h][:], size[t][:].indirect(n3_t[:, entries(h)]), twin[t, h][:], ALU.add)
 
-        def invert(t, h):
-            root = ring.tile([P, BANK], F32, name="root")
-            nc.scalar.activation(root[:], total[t, h][:], ACT.Abs_reciprocal_sqrt, bias=0.5)
-            recip[t, h] = keep.tile([P, BANK], F32, name="recip%d%d" % (t, h))
-            nc.scalar.activation(recip[t, h][:], root[:], ACT.Square)
+        def inverse_root(t, h):
+            root[t, h] = ring.tile([P, BANK], F32, name="root", bufs=3)
+            nc.scalar.activation(root[t, h][:], total[t, h][:], ACT.Abs_reciprocal_sqrt, bias=0.5)
 
         def finish(t, h):
+            recip = keep.tile([P, BANK], F32, name="recip%d%d" % (t, h))
+            nc.scalar.activation(recip[:], root[t, h][:], ACT.Square)
             res = ring.tile([P, BANK], F32, name="res", bufs=4)
             cuts = (0, 384, BANK) if (t, h) == (PACK - 1, HALVES - 1) else (0, BANK)
-            for first, end in zip(cuts, cuts[1:]):
-                lo, width = h * BANK + first, end - first
-                part = slice(first, end)
+            for start, end in zip(cuts, cuts[1:]):
+                lo, hi = h * BANK + start, h * BANK + end
+                part = slice(start, end)
                 nc.vector.tensor_tensor(
-                    res[:, part],
-                    signed[t][:].indirect(n2_t[:, lo // LANES : (lo + width) // LANES]),
-                    recip[t, h][:, part],
-                    ALU.mult,
+                    res[:, part], signed[t][:].indirect(n2_t[:, lo // LANES : hi // LANES]), recip[:, part], ALU.mult
                 )
-                nc.sync.dma_start(out_rows[t][:, :, lo : lo + width], res[:, part])
+                nc.sync.dma_start(out_rows[t][:, :, lo:hi], res[:, part])
 
         def twin_by_dma(t, h):
             nc.sync.dma_start(twin[t, h][:], size[t][:, half(h)])
 
         nc.vector.tensor_copy(twin[0, 0][:], size[0][:, half(0)])
         gather_total(0, 0)
+        nc.vector.tensor_copy(twin[0, 1][:], size[0][:, half(1)])
         sizes(1, 0)
         nc.vector.tensor_copy(twin[1, 0][:], size[1][:, half(0)])
-        nc.scalar.copy(twin[0, 1][:], size[0][:, half(1)])
         gather_total(0, 1)
         for t in range(1, PACK):
             for h in range(HALVES):
@@ -270,10 +271,16 @@ def tile_picked_candpagetnorm2_none_p_kernel(
             nc.scalar.activation(
                 signed[0][:, half(h)][:, QUARTER:], first[1, h][:, :QUARTER], ACT.Copy, scale=0.0625
             )
-        for t in range(PACK):
-            for h in range(HALVES):
-                if t > 0:
-                    signs(t, h)
-            for h in range(HALVES):
-                invert(t, h)
-                finish(t, h)
+        last = PACK - 1
+        for t in range(last):
+            inverse_root(t, 0)
+            inverse_root(t, 1)
+            finish(t, 0)
+            signs(t + 1, 0)
+            finish(t, 1)
+            if t + 1 == last:
+                inverse_root(last, 0)
+            signs(t + 1, 1)
+        finish(last, 0)
+        inverse_root(last, 1)
+        finish(last, 1)

from contextlib import ExitStack

import concourse.mybir as mybir

K, T, S, H, U, C = 512, 2048, 512, 512, 1024, 512
FLOPS = 2 * K * H * S + 2 * K * C * U

F32 = mybir.dt.float32
BF16 = mybir.dt.bfloat16
I32 = mybir.dt.int32
U32 = mybir.dt.uint32
U16 = mybir.dt.uint16
U8 = mybir.dt.uint8
FP8X4 = mybir.dt.float8_e4m3fn_x4
ACT = mybir.ActivationFunctionType
ALU = mybir.AluOpType

P = 128
PACK = 4
BANK = 512
HALVES = U // BANK
LANES = 16


def tile_picked_candpagetnorm2_none_p_kernel(
    tc, x_words, x_scales, w1, mem, gs, offs, n1, cand, n2, n3, out
):
    nc = tc.nc
    with ExitStack() as ctx:
        keep = ctx.enter_context(tc.tile_pool(name="keep", bufs=1))
        ring = ctx.enter_context(tc.tile_pool(name="ring", bufs=2))
        psum = ctx.enter_context(tc.psum_pool(name="psum", bufs=1))

        def bank(b):
            return psum.tile([P, BANK], F32, name="bank%d" % b, tag="bank%d" % b)

        def half(h):
            return slice(h * BANK, (h + 1) * BANK)

        offs_t = keep.tile([P, S // LANES], U16, name="offs_t")
        n1_t = keep.tile([P, S // LANES], U16, name="n1_t")
        cand_t = keep.tile([P, C // LANES], U16, name="cand_t")
        n2_t = keep.tile([P, U // LANES], U16, name="n2_t")
        n3_t = keep.tile([P, U // LANES], U16, name="n3_t")
        xw = keep.tile([P, T], U32, name="xw", align_bytes=64)
        xs = keep.tile([P, T], U8, name="xs", align_bytes=64)
        w_raw = [keep.tile([P, PACK, H // 2], F32, name="w_raw%d" % h) for h in range(2)]
        page = [keep.tile([P, U], F32, name="page%d" % t) for t in range(PACK)]
        gain = keep.tile([P, PACK], F32, name="gain")
        one = keep.tile([P, 1], F32, name="one")
        warm = keep.tile([P, 1], F32, name="warm")
        order = (2, 0, 1, 3)

        nc.vector.memset(xs[:].bitcast(I32), 0)
        nc.gpsimd.memset(one[:], 1.0)

        nc.sync.dma_start(offs_t[:], offs)
        nc.sync.dma_start(cand_t[:], cand)
        nc.sync.dma_start(n1_t[:], n1)
        for q in range(4):
            nc.sync.dma_start(
                xs[32 * q : 32 * q + 4, :].bitcast(I32), x_scales[0, 4 * q : 4 * q + 4, :].bitcast(I32)
            )
        nc.sync.dma_start(xw[:].bitcast(I32), x_words[0].rearrange("p n t -> p (n t)").bitcast(I32))
        nc.scalar.activation(warm[:], one[:], ACT.Silu)
        w_rows = w1.rearrange("(p j) c -> p j c", j=PACK)
        for h in range(2):
            nc.sync.dma_start(w_raw[h][:], w_rows[:, :, h * (H // 2) : (h + 1) * (H // 2)])
        mem_rows = mem.rearrange("(p t) w -> t p w", t=PACK)
        for t in order:
            nc.sync.dma_start(page[t][:], mem_rows[t])
        nc.sync.dma_start(gain[:], gs.rearrange("(p t) o -> p (t o)", t=PACK))
        nc.sync.dma_start(n3_t[:], n3)
        nc.sync.dma_start(n2_t[:], n2)

        xq_w = keep.tile([P, S], U32, name="xq_w", align_bytes=64)
        xq_s = keep.tile([P, S], U8, name="xq_s", align_bytes=64)
        cand_raw = keep.tile([P, C], U8, name="cand_raw", align_bytes=64)
        cand_s = keep.tile([P, C], U8, name="cand_s", align_bytes=64)
        cand_w = keep.tile([P, C], U32, name="cand_w", align_bytes=64)
        nc.vector.tensor_copy(xq_s[:], xs[:].indirect(offs_t[:]))
        nc.vector.tensor_copy(cand_raw[:], xs[:].indirect(cand_t[:]))
        nc.vector.tensor_copy(xq_w[:], xw[:].indirect(offs_t[:]))
        nc.vector.tensor_copy(
            cand_w[:].rearrange("p (t b e) -> p b t e", t=PACK, e=PACK), xw[:].indirect(cand_t[:])
        )
        nc.vector.tensor_copy(
            cand_s[:].bitcast(I32).rearrange("p (t b) -> p b t", t=PACK),
            cand_raw[:].bitcast(I32).rearrange("p (b t) -> p b t", t=PACK),
        )

        w_bf = keep.tile([P, PACK, P, PACK], BF16, name="w_bf", align_bytes=64)

        def weave(copy, h, lo, hi):
            copy(
                w_bf[:, :, h * (P // 2) + lo : h * (P // 2) + hi, :].rearrange("p t m j -> p m j t"),
                w_raw[h][:, :, lo * PACK : hi * PACK].rearrange("p j (m t) -> p m j t", t=PACK),
            )

        weave(nc.scalar.copy, 0, 0, P // 2)
        weave(nc.scalar.copy, 1, 0, P // 4)
        weave(nc.vector.tensor_copy, 1, P // 4, P // 2)
        w_codes = keep.tile([P, H], U32, name="w_codes", align_bytes=64)
        w_scales = keep.tile([P, H], U8, name="w_scales", align_bytes=64)
        for lo, hi in ((2, 3), (0, 2), (3, 4)):
            nc.vector.quantize_mx(
                out=w_codes[:, lo * P : hi * P].bitcast(FP8X4),
                scales=w_scales[:, lo * P : hi * P],
                in_=w_bf[:, lo:hi].rearrange("p t m j -> p (t m j)"),
            )

        y, th, fresh, kept = {}, {}, {}, {}
        for t in order:
            y[t] = bank(t)
            cols = slice(t * P, (t + 1) * P)
            nc.tensor.matmul_mx(
                out=y[t][:],
                lhsT=w_codes[:, cols].bitcast(FP8X4),
                lhsT_scale=w_scales[:, cols],
                rhs=xq_w[:].bitcast(FP8X4),
                rhs_scale=xq_s[:],
                start=True,
                stop=True,
            )
        z_bf = [keep.tile([P, BANK, PACK], BF16, name="z_bf%d" % h, align_bytes=64) for h in range(HALVES)]

        def gate(t):
            th[t] = keep.tile([P, S], F32, name="th%d" % t)
            nc.scalar.activation(th[t][:], y[t][:], ACT.Tanh, scale=-0.5)

        def new_part(t):
            fresh[t] = keep.tile([P, S], F32, name="fresh%d" % t)
            nc.scalar.activation(fresh[t][:], y[t][:], ACT.Silu)

        def old_part(t):
            hold = keep.tile([P, S], F32, name="hold%d" % t)
            nc.scalar.activation(hold[:], th[t][:], ACT.Copy, scale=0.5, bias=0.5)
            kept[t] = keep.tile([P, S], F32, name="kept%d" % t)
            nc.vector.tensor_tensor(kept[t][:], page[t][:].indirect(n1_t[:]), hold[:], ALU.mult)

        def put(t):
            nc.vector.tensor_tensor(page[t][:].indirect(n1_t[:]), kept[t][:], fresh[t][:], ALU.add)

        def plane(t, h):
            nc.scalar.activation(z_bf[h][:, :, t], page[t][:, half(h)], ACT.Copy, scale=gain[:, t : t + 1])

        a, b, c, d = order
        gate(a)
        new_part(a)
        half_old = keep.tile([P, S], F32, name="half_old")
        kept[a] = keep.tile([P, S], F32, name="kept_first")
        nc.vector.tensor_scalar(half_old[:], page[a][:].indirect(n1_t[:]), 0.5, 0.0, ALU.mult, ALU.add)
        nc.vector.scalar_tensor_tensor(kept[a][:], th[a][:], 1.0, half_old[:], ALU.add, ALU.mult)
        put(a)
        gate(b)
        gate(c)
        old_part(b)
        old_part(c)
        gate(d)
        new_part(b)
        put(b)
        old_part(d)
        plane(a, 0)
        plane(a, 1)
        new_part(c)
        put(c)
        new_part(d)
        put(d)
        for t in (b, c):
            for h in range(HALVES):
                plane(t, h)
        t = order[-1]
        QUARTER = BANK // 2
        for c in range(2):
            part = slice(c * QUARTER, (c + 1) * QUARTER)
            nc.vector.tensor_scalar(z_bf[0][:, part, t], page[t][:, half(0)][:, part], gain[:, t : t + 1], None, ALU.mult)
            nc.scalar.activation(z_bf[1][:, part, t], page[t][:, half(1)][:, part], ACT.Copy, scale=gain[:, t : t + 1])
        z_codes = [keep.tile([P, BANK], U32, name="z_codes%d" % h, align_bytes=64) for h in range(HALVES)]
        z_scales = [keep.tile([P, BANK], U8, name="z_scales%d" % h, align_bytes=64) for h in range(HALVES)]
        for c in range(2):
            part = slice(c * QUARTER, (c + 1) * QUARTER)
            for h in range(HALVES):
                nc.vector.quantize_mx(
                    out=z_codes[h][:, part].bitcast(FP8X4),
                    scales=z_scales[h][:, part],
                    in_=z_bf[h][:, part, :].rearrange("p w t -> p (w t)"),
                )

        out_rows = out.rearrange("(b t e) w -> t b e w", t=PACK, e=PACK)
        size = [keep.tile([P, U], F32, name="size%d" % t) for t in range(PACK)]
        signed = [keep.tile([P, U], F32, name="signed%d" % t) for t in range(PACK)]
        acc, twin, total, root = {}, {}, {}, {}
        for t in range(PACK):
            for h in range(HALVES):
                twin[t, h] = keep.tile([P, BANK], F32, name="twin%d%d" % (t, h))

        def score(result, t, h, part):
            cols = slice(t * P, (t + 1) * P)
            nc.tensor.matmul_mx(
                out=result,
                lhsT=cand_w[:, cols].bitcast(FP8X4),
                lhsT_scale=cand_s[:, cols],
                rhs=z_codes[h][:, part].bitcast(FP8X4),
                rhs_scale=z_scales[h][:, part],
                start=True,
                stop=True,
            )

        first = {}
        for c in range(2):
            part = slice(c * QUARTER, (c + 1) * QUARTER)
            for h in range(HALVES):
                first[c, h] = bank(2 * c + h)
                score(first[c, h][:, :QUARTER], 0, h, part)
                nc.scalar.activation(size[0][:, half(h)][:, part], first[c, h][:, :QUARTER], ACT.Abs, scale=0.0625)
        for h in range(HALVES):
            nc.vector.tensor_scalar(signed[0][:, half(h)][:, :QUARTER], first[0, h][:, :QUARTER], 0.0625, None, ALU.mult)
        for t in range(1, PACK):
            for h in range(HALVES):
                acc[t, h] = bank((2 * t + 2 + h) % 8)
                score(acc[t, h][:], t, h, slice(0, BANK))

        def entries(h):
            return slice(h * BANK // LANES, (h + 1) * BANK // LANES)

        def sizes(t, h):
            nc.scalar.activation(size[t][:, half(h)], acc[t, h][:], ACT.Abs, scale=0.0625)

        def signs(t, h):
            nc.scalar.activation(signed[t][:, half(h)], acc[t, h][:], ACT.Copy, scale=0.0625)

        def gather_total(t, h):
            total[t, h] = keep.tile([P, BANK], F32, name="total%d%d" % (t, h))
            nc.vector.tensor_tensor(total[t, h][:], size[t][:].indirect(n3_t[:, entries(h)]), twin[t, h][:], ALU.add)

        def inverse_root(t, h):
            root[t, h] = ring.tile([P, BANK], F32, name="root", bufs=3)
            nc.scalar.activation(root[t, h][:], total[t, h][:], ACT.Abs_reciprocal_sqrt, bias=0.5)

        def finish(t, h):
            recip = keep.tile([P, BANK], F32, name="recip%d%d" % (t, h))
            nc.scalar.activation(recip[:], root[t, h][:], ACT.Square)
            res = ring.tile([P, BANK], F32, name="res", bufs=4)
            cuts = (0, 384, BANK) if (t, h) == (PACK - 1, HALVES - 1) else (0, BANK)
            for start, end in zip(cuts, cuts[1:]):
                lo, hi = h * BANK + start, h * BANK + end
                part = slice(start, end)
                nc.vector.tensor_tensor(
                    res[:, part], signed[t][:].indirect(n2_t[:, lo // LANES : hi // LANES]), recip[:, part], ALU.mult
                )
                nc.sync.dma_start(out_rows[t][:, :, lo:hi], res[:, part])

        def twin_by_dma(t, h):
            nc.sync.dma_start(twin[t, h][:], size[t][:, half(h)])

        nc.vector.tensor_copy(twin[0, 0][:], size[0][:, half(0)])
        gather_total(0, 0)
        nc.vector.tensor_copy(twin[0, 1][:], size[0][:, half(1)])
        sizes(1, 0)
        nc.vector.tensor_copy(twin[1, 0][:], size[1][:, half(0)])
        gather_total(0, 1)
        for t in range(1, PACK):
            for h in range(HALVES):
                if (t, h) != (1, 0):
                    sizes(t, h)
                    twin_by_dma(t, h)
        for t in range(1, PACK):
            for h in range(HALVES):
                gather_total(t, h)
        for h in range(HALVES):
            nc.scalar.activation(
                signed[0][:, half(h)][:, QUARTER:], first[1, h][:, :QUARTER], ACT.Copy, scale=0.0625
            )
        last = PACK - 1
        for t in range(last):
            inverse_root(t, 0)
            inverse_root(t, 1)
            finish(t, 0)
            signs(t + 1, 0)
            finish(t, 1)
            if t + 1 == last:
                inverse_root(last, 0)
            signs(t + 1, 1)
        finish(last, 0)
        inverse_root(last, 1)
        finish(last, 1)
